import numpy as np, ml_dtypes
CORES = [6,14,22,30,38,134,142,150,158]
N = 9
import mx_ref
NC, G, D = 384, 2, 16
C = np.float32(0.031)
BF = ml_dtypes.bfloat16
def cut(t, i, w=512):
    return t[:, w * i:w * i + w]
def tile(rs):
    return np.stack(rs, axis=2).reshape(128, -1).astype(BF)
def act(Z):
    return [np.maximum(s * z, 0) * C for z in Z for s in (1, -1)]
def taps(w, i, e):
    return mx_ref.matmul(mx_ref.quantize(cut(w, 2 * i)), mx_ref.quantize(e[:, :4 * NC])) + mx_ref.matmul(mx_ref.quantize(cut(w, 2 * i + 1)), mx_ref.quantize(e[:, 4 * D:4 * D + 4 * NC]))
def setup_inputs(rng):
    def f(*shape):
        return mx_ref.flush((rng.standard_normal(shape, dtype=np.float32) * np.exp2(rng.integers(-2, 3, shape[:-1] + (1,)))).astype(BF))
    return {"x": f(N, 128, 4 * NC), "wa": np.broadcast_to(f(1, 128, 2 * G * 512), (N, 128, 2 * G * 512)).copy(), "wb": f(N, 128, 2 * 512)}
def setup_inputs_blocks(rng):
    d = setup_inputs(rng)
    for k in ("x", "wb"): d[k] = mx_ref.spread(d[k], rng, 2)
    return d
def setup_inputs_wide(rng):
    d = setup_inputs(rng)
    for k in ("wb",): d[k] = mx_ref.flush((d[k].astype(np.float32) * np.exp2(rng.integers(-6, 7, (N, 1, 1))).astype(np.float32)).astype(BF))
    return d
def setup_inputs_zeros(rng):
    d = setup_inputs(rng); v = d["x"].reshape(N, 128, -1, 4).copy()
    v[np.broadcast_to((rng.random((N, 1, v.shape[2], 1)) < 0.33), v.shape)] = 0
    d["x"] = v.reshape(d["x"].shape)
    return d
def reference(x, wa, wb):
    edge = lambda t, r: np.concatenate([t[(r - 1) % N][:, 4 * (NC - D):], t[r]], axis=1)
    u = [tile(act([taps(wa[r], i, edge(x, r)) for i in range(G)])) for r in range(N)]
    y = np.zeros((N, 128, NC), np.float32)
    for r in range(N):
        y[r] = taps(wb[r], 0, edge(u, r))
    return {"y": y}

@@ -1,0 +1,150 @@
+from concourse.mybir import dt, AluOpType, ActivationFunctionType
+
+NC, D = 384, 16
+HALO = 2 * D
+XE, UE = NC + HALO, NC + D
+C = 0.031
+TAIL = 128
+MID = 216
+YMID = MID - D
+UB = TAIL + D
+
+SCRATCH = {
+    "xs": ("sbuf", [128, 4 * NC], "bfloat16"),
+    "was": ("sbuf", [128, 2048], "bfloat16"),
+    "wbs": ("sbuf", [128, 1024], "bfloat16"),
+    "qx": ("sbuf", [128, XE], "float8_e4m3fn_x4"),
+    "sx": ("sbuf", [128, XE], "uint8"),
+    "qa": ("sbuf", [128, 512], "float8_e4m3fn_x4"),
+    "sa": ("sbuf", [128, 512], "uint8"),
+    "qb": ("sbuf", [128, 256], "float8_e4m3fn_x4"),
+    "sb": ("sbuf", [128, 256], "uint8"),
+    "u": ("sbuf", [128, 4 * UE], "bfloat16"),
+    "qu": ("sbuf", [128, UE], "float8_e4m3fn_x4"),
+    "su": ("sbuf", [128, UE], "uint8"),
+    "qub": ("sbuf", [128, UB], "float8_e4m3fn_x4"),
+    "sub": ("sbuf", [128, UB], "uint8"),
+    "ys": ("sbuf", [128, NC], "float32"),
+    "z0lo": ("psum", [128, 512], "float32"),
+    "z0hi": ("psum", [128, 512], "float32"),
+    "z1lo": ("psum", [128, 512], "float32"),
+    "z1hi": ("psum", [128, 512], "float32"),
+    "z0b": ("psum", [128, 512], "float32"),
+    "z1b": ("psum", [128, 512], "float32"),
+    "yb": ("psum", [128, 512], "float32"),
+}
+SEMAPHORES = ["ld_xt", "ld_xh", "ld_wa0", "ld_wa1", "ld_wb", "q_xt", "q_xh", "q_wa0", "q_wa1", "q_wb",
+              "m0lo", "m0hi", "m1lo", "m1hi", "a0lo", "a0hi", "a1lo", "a1hi", "qu_lo", "qu_hi", "mylo", "myhi", "cylo", "cyhi",
+              "arr", "sent", "m0b", "m1b", "a0b", "a1b", "q_b", "myb", "cyb", "st", "stb"]
+
+
+def rank_program(g, core, T, topo):
+    rank = T.rank_of(core)
+    if rank is None:
+        return
+    s = T.sem
+    te, ve, sc, sy = g.tensor, g.vector, g.scalar, g.sync
+    H4 = 4 * (NC - TAIL)
+
+    sy.dma_start(T.xs[0:64, H4:], T.x[0:64, H4:]).then_inc(s.ld_xt, 16)
+    sc.dma_start(T.xs[64:128, H4:], T.x[64:128, H4:]).then_inc(s.ld_xt, 16)
+    sy.dma_start(T.xs[:, 0:H4], T.x[:, 0:H4]).then_inc(s.ld_xh, 16)
+    sc.dma_start(T.was[:, 0:1024], T.wa[:, 0:1024]).then_inc(s.ld_wa0, 16)
+    sy.dma_start(T.was[0:64, 1024:2048], T.wa[0:64, 1024:2048]).then_inc(s.ld_wa1, 16)
+    sc.dma_start(T.was[64:128, 1024:2048], T.wa[64:128, 1024:2048]).then_inc(s.ld_wa1, 16)
+    sy.wait_ge(s.ld_xt, 32)
+    sy.dma_start(T.wbs[:], T.wb[:]).then_inc(s.ld_wb, 16)
+
+    dst = T.cores[(rank + 1) % len(T.cores)]
+    rid, pid = topo.addr(dst, core)
+    allowed = [e for e in range(16) if topo.mask(core, dst) >> e & 1]
+    engines = allowed[::2]
+    mask, n_eng = sum(1 << e for e in engines), len(engines)
+    g.wait_ge(s.q_xt, 1)
+    g.remote_dma(T.qx[:, 0:HALO].bitcast(dt.uint8), T.qx[:, NC:XE].bitcast(dt.uint8), s.arr, s.sent, pid, rid, mask)
+    g.remote_dma(T.sx[:, 0:HALO], T.sx[:, NC:XE], s.arr, s.sent, pid, rid, mask)
+    g.wait_ge(s.sent, 2 * n_eng)
+
+    def mm2(bank, n, w, ws, k, q, qs, a, sem):
+        for t in range(2):
+            c0, w0 = a + t * D, 128 * (k + t)
+            i = te.matmul_mx(bank[:, 0:n], w[:, w0:w0 + 128], ws[:, w0:w0 + 128], q[:, c0:c0 + n], qs[:, c0:c0 + n], t == 0, t == 1)
+        i.then_inc(sem, 1)
+
+    def uview(i, sgn, a, b):
+        return T.u[:, 4 * a + 2 * i + sgn:4 * b:4]
+
+    def act_s(bank, i, a, b, sem):
+        for sgn in range(2):
+            sc.activation(uview(i, sgn, a, b), bank[:, 0:b - a], ActivationFunctionType.Relu, scale=-C if sgn else C).then_inc(sem, 1)
+
+    def act_v(bank, i, a, b, sem):
+        for sgn in range(2):
+            ve.tensor_scalar(uview(i, sgn, a, b), bank[:, 0:b - a], -C if sgn else C, 0.0, AluOpType.mult, AluOpType.max).then_inc(sem, 1)
+
+    te.wait_ge(s.q_wa0, 1)
+    te.wait_ge(s.q_xh, 1)
+    mm2(T.z0lo, MID - HALO, T.qa, T.sa, 0, T.qx, T.sx, HALO, s.m0lo)
+    te.wait_ge(s.q_xt, 1)
+    mm2(T.z0hi, UE - MID, T.qa, T.sa, 0, T.qx, T.sx, MID, s.m0hi)
+    te.wait_ge(s.q_wa1, 1)
+    mm2(T.z1lo, MID - HALO, T.qa, T.sa, 2, T.qx, T.sx, HALO, s.m1lo)
+    mm2(T.z1hi, UE - MID, T.qa, T.sa, 2, T.qx, T.sx, MID, s.m1hi)
+    te.wait_ge(s.q_wb, 1)
+    te.wait_ge(s.qu_lo, 1)
+    mm2(T.z0lo, YMID - HALO, T.qb, T.sb, 0, T.qu, T.su, HALO, s.mylo)
+    te.wait_ge(s.qu_hi, 1)
+    mm2(T.z0hi, NC - YMID, T.qb, T.sb, 0, T.qu, T.su, YMID, s.myhi)
+    te.wait_ge(s.arr, 2 * n_eng)
+    mm2(T.z0b, TAIL, T.qa, T.sa, 0, T.qx, T.sx, 0, s.m0b)
+    mm2(T.z1b, TAIL, T.qa, T.sa, 2, T.qx, T.sx, 0, s.m1b)
+    te.wait_ge(s.q_b, 1)
+    mm2(T.yb, TAIL, T.qb, T.sb, 0, T.qub, T.sub, 0, s.myb)
+
+    sc.wait_ge(s.m0lo, 1)
+    act_s(T.z0lo, 0, HALO, MID, s.a0lo)
+    sc.wait_ge(s.m0hi, 1)
+    act_s(T.z0hi, 0, MID, UE, s.a0hi)
+    sc.wait_ge(s.m1hi, 1)
+    act_s(T.z1hi, 1, MID, UE, s.a1hi)
+    sc.wait_ge(s.mylo, 1)
+    sc.activation(T.ys[:, HALO:YMID], T.z0lo[:, 0:YMID - HALO], ActivationFunctionType.Copy).then_inc(s.cylo, 1)
+    sc.wait_ge(s.m0b, 1)
+    act_s(T.z0b, 0, 0, HALO, s.a0b)
+    sc.wait_ge(s.cyb, 1)
+    sc.dma_start(T.y[:, 0:HALO], T.ys[:, 0:HALO]).then_inc(s.stb, 16)
+    sc.wait_ge(s.stb, 16)
+
+    ve.wait_ge(s.ld_xt, 32)
+    ve.quantize_mx(T.qx[:, XE - TAIL:XE], T.sx[:, XE - TAIL:XE], T.xs[:, H4:4 * NC]).then_inc(s.q_xt, 1)
+    ve.wait_ge(s.ld_xh, 16)
+    ve.quantize_mx(T.qx[:, HALO:XE - TAIL], T.sx[:, HALO:XE - TAIL], T.xs[:, 0:H4]).then_inc(s.q_xh, 1)
+    ve.wait_ge(s.ld_wa0, 16)
+    ve.quantize_mx(T.qa[:, 0:256], T.sa[:, 0:256], T.was[:, 0:1024]).then_inc(s.q_wa0, 1)
+    ve.wait_ge(s.ld_wa1, 32)
+    ve.quantize_mx(T.qa[:, 256:512], T.sa[:, 256:512], T.was[:, 1024:2048]).then_inc(s.q_wa1, 1)
+    ve.wait_ge(s.m1lo, 1)
+    act_v(T.z1lo, 1, HALO, MID, s.a1lo)
+    ve.wait_ge(s.ld_wb, 16)
+    ve.quantize_mx(T.qb[:], T.sb[:], T.wbs[:]).then_inc(s.q_wb, 1)
+    ve.wait_ge(s.a0lo, 2)
+    ve.wait_ge(s.a1lo, 2)
+    ve.quantize_mx(T.qu[:, HALO:MID], T.su[:, HALO:MID], T.u[:, 4 * HALO:4 * MID]).then_inc(s.qu_lo, 1)
+    ve.wait_ge(s.a0hi, 2)
+    ve.wait_ge(s.a1hi, 2)
+    ve.quantize_mx(T.qu[:, MID:UE], T.su[:, MID:UE], T.u[:, 4 * MID:4 * UE]).then_inc(s.qu_hi, 1)
+    ve.wait_ge(s.myhi, 1)
+    ve.tensor_copy(T.ys[:, YMID:NC], T.z0hi[:, 0:NC - YMID]).then_inc(s.cyhi, 1)
+    ve.wait_ge(s.m1b, 1)
+    act_v(T.z1b, 1, 0, HALO, s.a1b)
+    ve.wait_ge(s.a0b, 2)
+    ve.wait_ge(s.a1b, 2)
+    ve.quantize_mx(T.qub[:], T.sub[:], T.u[:, 0:4 * UB]).then_inc(s.q_b, 1)
+    ve.wait_ge(s.myb, 1)
+    ve.tensor_copy(T.ys[:, 0:HALO], T.yb[:, 0:HALO]).then_inc(s.cyb, 1)
+
+    sy.wait_ge(s.cylo, 1)
+    sy.dma_start(T.y[:, HALO:YMID], T.ys[:, HALO:YMID]).then_inc(s.st, 16)
+    sy.wait_ge(s.cyhi, 1)
+    sy.dma_start(T.y[:, YMID:NC], T.ys[:, YMID:NC]).then_inc(s.st, 16)
+    sy.wait_ge(s.st, 32)

@@ -5,7 +5,7 @@ HALO = 2 * D
 XE, UE = NC + HALO, NC + D
 C = 0.031
 TAIL = 128
-MID = 216
+MID = 208
 YMID = MID - D
 UB = TAIL + D
 
@@ -57,9 +57,8 @@ def rank_program(g, core, T, topo):
 
     dst = T.cores[(rank + 1) % len(T.cores)]
     rid, pid = topo.addr(dst, core)
-    allowed = [e for e in range(16) if topo.mask(core, dst) >> e & 1]
-    engines = allowed[::2]
-    mask, n_eng = sum(1 << e for e in engines), len(engines)
+    mask = topo.mask(core, dst)
+    n_eng = bin(mask).count("1")
     g.wait_ge(s.q_xt, 1)
     g.remote_dma(T.qx[:, 0:HALO].bitcast(dt.uint8), T.qx[:, NC:XE].bitcast(dt.uint8), s.arr, s.sent, pid, rid, mask)
     g.remote_dma(T.sx[:, 0:HALO], T.sx[:, NC:XE], s.arr, s.sent, pid, rid, mask)
@@ -90,27 +89,25 @@ def rank_program(g, core, T, topo):
     te.wait_ge(s.q_wa1, 1)
     mm2(T.z1lo, MID - HALO, T.qa, T.sa, 2, T.qx, T.sx, HALO, s.m1lo)
     mm2(T.z1hi, UE - MID, T.qa, T.sa, 2, T.qx, T.sx, MID, s.m1hi)
+    te.wait_ge(s.arr, 2 * n_eng)
+    mm2(T.z0b, TAIL, T.qa, T.sa, 0, T.qx, T.sx, 0, s.m0b)
+    mm2(T.z1b, TAIL, T.qa, T.sa, 2, T.qx, T.sx, 0, s.m1b)
     te.wait_ge(s.q_wb, 1)
     te.wait_ge(s.qu_lo, 1)
     mm2(T.z0lo, YMID - HALO, T.qb, T.sb, 0, T.qu, T.su, HALO, s.mylo)
     te.wait_ge(s.qu_hi, 1)
     mm2(T.z0hi, NC - YMID, T.qb, T.sb, 0, T.qu, T.su, YMID, s.myhi)
-    te.wait_ge(s.arr, 2 * n_eng)
-    mm2(T.z0b, TAIL, T.qa, T.sa, 0, T.qx, T.sx, 0, s.m0b)
-    mm2(T.z1b, TAIL, T.qa, T.sa, 2, T.qx, T.sx, 0, s.m1b)
     te.wait_ge(s.q_b, 1)
     mm2(T.yb, TAIL, T.qb, T.sb, 0, T.qub, T.sub, 0, s.myb)
 
-    sc.wait_ge(s.m0lo, 1)
-    act_s(T.z0lo, 0, HALO, MID, s.a0lo)
     sc.wait_ge(s.m0hi, 1)
     act_s(T.z0hi, 0, MID, UE, s.a0hi)
     sc.wait_ge(s.m1hi, 1)
     act_s(T.z1hi, 1, MID, UE, s.a1hi)
-    sc.wait_ge(s.mylo, 1)
-    sc.activation(T.ys[:, HALO:YMID], T.z0lo[:, 0:YMID - HALO], ActivationFunctionType.Copy).then_inc(s.cylo, 1)
     sc.wait_ge(s.m0b, 1)
     act_s(T.z0b, 0, 0, HALO, s.a0b)
+    sc.wait_ge(s.mylo, 1)
+    sc.activation(T.ys[:, HALO:YMID], T.z0lo[:, 0:YMID - HALO], ActivationFunctionType.Copy).then_inc(s.cylo, 1)
     sc.wait_ge(s.cyb, 1)
     sc.dma_start(T.y[:, 0:HALO], T.ys[:, 0:HALO]).then_inc(s.stb, 16)
     sc.wait_ge(s.stb, 16)
@@ -123,23 +120,25 @@ def rank_program(g, core, T, topo):
     ve.quantize_mx(T.qa[:, 0:256], T.sa[:, 0:256], T.was[:, 0:1024]).then_inc(s.q_wa0, 1)
     ve.wait_ge(s.ld_wa1, 32)
     ve.quantize_mx(T.qa[:, 256:512], T.sa[:, 256:512], T.was[:, 1024:2048]).then_inc(s.q_wa1, 1)
+    ve.wait_ge(s.m0lo, 1)
+    act_v(T.z0lo, 0, HALO, MID, s.a0lo)
     ve.wait_ge(s.m1lo, 1)
     act_v(T.z1lo, 1, HALO, MID, s.a1lo)
-    ve.wait_ge(s.ld_wb, 16)
-    ve.quantize_mx(T.qb[:], T.sb[:], T.wbs[:]).then_inc(s.q_wb, 1)
     ve.wait_ge(s.a0lo, 2)
     ve.wait_ge(s.a1lo, 2)
     ve.quantize_mx(T.qu[:, HALO:MID], T.su[:, HALO:MID], T.u[:, 4 * HALO:4 * MID]).then_inc(s.qu_lo, 1)
+    ve.wait_ge(s.ld_wb, 16)
+    ve.quantize_mx(T.qb[:], T.sb[:], T.wbs[:]).then_inc(s.q_wb, 1)
     ve.wait_ge(s.a0hi, 2)
     ve.wait_ge(s.a1hi, 2)
     ve.quantize_mx(T.qu[:, MID:UE], T.su[:, MID:UE], T.u[:, 4 * MID:4 * UE]).then_inc(s.qu_hi, 1)
-    ve.wait_ge(s.myhi, 1)
-    ve.tensor_copy(T.ys[:, YMID:NC], T.z0hi[:, 0:NC - YMID]).then_inc(s.cyhi, 1)
     ve.wait_ge(s.m1b, 1)
     act_v(T.z1b, 1, 0, HALO, s.a1b)
     ve.wait_ge(s.a0b, 2)
     ve.wait_ge(s.a1b, 2)
     ve.quantize_mx(T.qub[:], T.sub[:], T.u[:, 0:4 * UB]).then_inc(s.q_b, 1)
+    ve.wait_ge(s.myhi, 1)
+    ve.tensor_copy(T.ys[:, YMID:NC], T.z0hi[:, 0:NC - YMID]).then_inc(s.cyhi, 1)
     ve.wait_ge(s.myb, 1)
     ve.tensor_copy(T.ys[:, 0:HALO], T.yb[:, 0:HALO]).then_inc(s.cyb, 1)
 

from concourse.mybir import dt, AluOpType, ActivationFunctionType

NC, D = 384, 16
HALO = 2 * D
XE, UE = NC + HALO, NC + D
C = 0.031
TAIL = 128
MID = 208
YMID = MID - D
UB = TAIL + D

SCRATCH = {
    "xs": ("sbuf", [128, 4 * NC], "bfloat16"),
    "was": ("sbuf", [128, 2048], "bfloat16"),
    "wbs": ("sbuf", [128, 1024], "bfloat16"),
    "qx": ("sbuf", [128, XE], "float8_e4m3fn_x4"),
    "sx": ("sbuf", [128, XE], "uint8"),
    "qa": ("sbuf", [128, 512], "float8_e4m3fn_x4"),
    "sa": ("sbuf", [128, 512], "uint8"),
    "qb": ("sbuf", [128, 256], "float8_e4m3fn_x4"),
    "sb": ("sbuf", [128, 256], "uint8"),
    "u": ("sbuf", [128, 4 * UE], "bfloat16"),
    "qu": ("sbuf", [128, UE], "float8_e4m3fn_x4"),
    "su": ("sbuf", [128, UE], "uint8"),
    "qub": ("sbuf", [128, UB], "float8_e4m3fn_x4"),
    "sub": ("sbuf", [128, UB], "uint8"),
    "ys": ("sbuf", [128, NC], "float32"),
    "z0lo": ("psum", [128, 512], "float32"),
    "z0hi": ("psum", [128, 512], "float32"),
    "z1lo": ("psum", [128, 512], "float32"),
    "z1hi": ("psum", [128, 512], "float32"),
    "z0b": ("psum", [128, 512], "float32"),
    "z1b": ("psum", [128, 512], "float32"),
    "yb": ("psum", [128, 512], "float32"),
}
SEMAPHORES = ["ld_xt", "ld_xh", "ld_wa0", "ld_wa1", "ld_wb", "q_xt", "q_xh", "q_wa0", "q_wa1", "q_wb",
              "m0lo", "m0hi", "m1lo", "m1hi", "a0lo", "a0hi", "a1lo", "a1hi", "qu_lo", "qu_hi", "mylo", "myhi", "cylo", "cyhi",
              "arr", "sent", "m0b", "m1b", "a0b", "a1b", "q_b", "myb", "cyb", "st", "stb"]


def rank_program(g, core, T, topo):
    rank = T.rank_of(core)
    if rank is None:
        return
    s = T.sem
    te, ve, sc, sy = g.tensor, g.vector, g.scalar, g.sync
    H4 = 4 * (NC - TAIL)

    sy.dma_start(T.xs[0:64, H4:], T.x[0:64, H4:]).then_inc(s.ld_xt, 16)
    sc.dma_start(T.xs[64:128, H4:], T.x[64:128, H4:]).then_inc(s.ld_xt, 16)
    sy.dma_start(T.xs[:, 0:H4], T.x[:, 0:H4]).then_inc(s.ld_xh, 16)
    sc.dma_start(T.was[:, 0:1024], T.wa[:, 0:1024]).then_inc(s.ld_wa0, 16)
    sy.dma_start(T.was[0:64, 1024:2048], T.wa[0:64, 1024:2048]).then_inc(s.ld_wa1, 16)
    sc.dma_start(T.was[64:128, 1024:2048], T.wa[64:128, 1024:2048]).then_inc(s.ld_wa1, 16)
    sy.wait_ge(s.ld_xt, 32)
    sy.dma_start(T.wbs[:], T.wb[:]).then_inc(s.ld_wb, 16)

    dst = T.cores[(rank + 1) % len(T.cores)]
    rid, pid = topo.addr(dst, core)
    mask = topo.mask(core, dst)
    n_eng = bin(mask).count("1")
    g.wait_ge(s.q_xt, 1)
    g.remote_dma(T.qx[:, 0:HALO].bitcast(dt.uint8), T.qx[:, NC:XE].bitcast(dt.uint8), s.arr, s.sent, pid, rid, mask)
    g.remote_dma(T.sx[:, 0:HALO], T.sx[:, NC:XE], s.arr, s.sent, pid, rid, mask)
    g.wait_ge(s.sent, 2 * n_eng)

    def mm2(bank, n, w, ws, k, q, qs, a, sem):
        for t in range(2):
            c0, w0 = a + t * D, 128 * (k + t)
            i = te.matmul_mx(bank[:, 0:n], w[:, w0:w0 + 128], ws[:, w0:w0 + 128], q[:, c0:c0 + n], qs[:, c0:c0 + n], t == 0, t == 1)
        i.then_inc(sem, 1)

    def uview(i, sgn, a, b):
        return T.u[:, 4 * a + 2 * i + sgn:4 * b:4]

    def act_s(bank, i, a, b, sem):
        for sgn in range(2):
            sc.activation(uview(i, sgn, a, b), bank[:, 0:b - a], ActivationFunctionType.Relu, scale=-C if sgn else C).then_inc(sem, 1)

    def act_v(bank, i, a, b, sem):
        for sgn in range(2):
            ve.tensor_scalar(uview(i, sgn, a, b), bank[:, 0:b - a], -C if sgn else C, 0.0, AluOpType.mult, AluOpType.max).then_inc(sem, 1)

    te.wait_ge(s.q_wa0, 1)
    te.wait_ge(s.q_xh, 1)
    mm2(T.z0lo, MID - HALO, T.qa, T.sa, 0, T.qx, T.sx, HALO, s.m0lo)
    te.wait_ge(s.q_xt, 1)
    mm2(T.z0hi, UE - MID, T.qa, T.sa, 0, T.qx, T.sx, MID, s.m0hi)
    te.wait_ge(s.q_wa1, 1)
    mm2(T.z1lo, MID - HALO, T.qa, T.sa, 2, T.qx, T.sx, HALO, s.m1lo)
    mm2(T.z1hi, UE - MID, T.qa, T.sa, 2, T.qx, T.sx, MID, s.m1hi)
    te.wait_ge(s.arr, 2 * n_eng)
    mm2(T.z0b, TAIL, T.qa, T.sa, 0, T.qx, T.sx, 0, s.m0b)
    mm2(T.z1b, TAIL, T.qa, T.sa, 2, T.qx, T.sx, 0, s.m1b)
    te.wait_ge(s.q_wb, 1)
    te.wait_ge(s.qu_lo, 1)
    mm2(T.z0lo, YMID - HALO, T.qb, T.sb, 0, T.qu, T.su, HALO, s.mylo)
    te.wait_ge(s.qu_hi, 1)
    mm2(T.z0hi, NC - YMID, T.qb, T.sb, 0, T.qu, T.su, YMID, s.myhi)
    te.wait_ge(s.q_b, 1)
    mm2(T.yb, TAIL, T.qb, T.sb, 0, T.qub, T.sub, 0, s.myb)

    sc.wait_ge(s.m0hi, 1)
    act_s(T.z0hi, 0, MID, UE, s.a0hi)
    sc.wait_ge(s.m1hi, 1)
    act_s(T.z1hi, 1, MID, UE, s.a1hi)
    sc.wait_ge(s.m0b, 1)
    act_s(T.z0b, 0, 0, HALO, s.a0b)
    sc.wait_ge(s.mylo, 1)
    sc.activation(T.ys[:, HALO:YMID], T.z0lo[:, 0:YMID - HALO], ActivationFunctionType.Copy).then_inc(s.cylo, 1)
    sc.wait_ge(s.cyb, 1)
    sc.dma_start(T.y[:, 0:HALO], T.ys[:, 0:HALO]).then_inc(s.stb, 16)
    sc.wait_ge(s.stb, 16)

    ve.wait_ge(s.ld_xt, 32)
    ve.quantize_mx(T.qx[:, XE - TAIL:XE], T.sx[:, XE - TAIL:XE], T.xs[:, H4:4 * NC]).then_inc(s.q_xt, 1)
    ve.wait_ge(s.ld_xh, 16)
    ve.quantize_mx(T.qx[:, HALO:XE - TAIL], T.sx[:, HALO:XE - TAIL], T.xs[:, 0:H4]).then_inc(s.q_xh, 1)
    ve.wait_ge(s.ld_wa0, 16)
    ve.quantize_mx(T.qa[:, 0:256], T.sa[:, 0:256], T.was[:, 0:1024]).then_inc(s.q_wa0, 1)
    ve.wait_ge(s.ld_wa1, 32)
    ve.quantize_mx(T.qa[:, 256:512], T.sa[:, 256:512], T.was[:, 1024:2048]).then_inc(s.q_wa1, 1)
    ve.wait_ge(s.m0lo, 1)
    act_v(T.z0lo, 0, HALO, MID, s.a0lo)
    ve.wait_ge(s.m1lo, 1)
    act_v(T.z1lo, 1, HALO, MID, s.a1lo)
    ve.wait_ge(s.a0lo, 2)
    ve.wait_ge(s.a1lo, 2)
    ve.quantize_mx(T.qu[:, HALO:MID], T.su[:, HALO:MID], T.u[:, 4 * HALO:4 * MID]).then_inc(s.qu_lo, 1)
    ve.wait_ge(s.ld_wb, 16)
    ve.quantize_mx(T.qb[:], T.sb[:], T.wbs[:]).then_inc(s.q_wb, 1)
    ve.wait_ge(s.a0hi, 2)
    ve.wait_ge(s.a1hi, 2)
    ve.quantize_mx(T.qu[:, MID:UE], T.su[:, MID:UE], T.u[:, 4 * MID:4 * UE]).then_inc(s.qu_hi, 1)
    ve.wait_ge(s.m1b, 1)
    act_v(T.z1b, 1, 0, HALO, s.a1b)
    ve.wait_ge(s.a0b, 2)
    ve.wait_ge(s.a1b, 2)
    ve.quantize_mx(T.qub[:], T.sub[:], T.u[:, 0:4 * UB]).then_inc(s.q_b, 1)
    ve.wait_ge(s.myhi, 1)
    ve.tensor_copy(T.ys[:, YMID:NC], T.z0hi[:, 0:NC - YMID]).then_inc(s.cyhi, 1)
    ve.wait_ge(s.myb, 1)
    ve.tensor_copy(T.ys[:, 0:HALO], T.yb[:, 0:HALO]).then_inc(s.cyb, 1)

    sy.wait_ge(s.cylo, 1)
    sy.dma_start(T.y[:, HALO:YMID], T.ys[:, HALO:YMID]).then_inc(s.st, 16)
    sy.wait_ge(s.cyhi, 1)
    sy.dma_start(T.y[:, YMID:NC], T.ys[:, YMID:NC]).then_inc(s.st, 16)
    sy.wait_ge(s.st, 32)
